import numpy as np
import ml_dtypes


def mxq(x, axis, fmt="e4m3"):
    dtype, down = {"e4m3": (ml_dtypes.float8_e4m3fn, 7), "e5m2": (ml_dtypes.float8_e5m2, 14)}[fmt]
    v = np.moveaxis(np.asarray(x, np.float32).astype(ml_dtypes.bfloat16).astype(np.float64), axis, -1)
    blocks = v.reshape(v.shape[:-1] + (-1, 32))
    amax = np.abs(blocks).max(-1, keepdims=True)
    byte = np.maximum(np.where(amax > 0, np.frexp(amax)[1] - 1 + 127, 0) - down, 1)
    scale = np.exp2(byte - 127.0)
    codes = (blocks / scale).astype(np.float32).astype(dtype).astype(np.float64)
    return np.moveaxis((codes * scale).reshape(v.shape), -1, axis)


WIDE = False


def mx_kscale(k):
    if not WIDE:
        return np.ones(k)
    levels = np.array([10, -10, 5, -5, 0])
    if k % 512:
        return np.exp2(np.random.permutation(np.resize(levels, k // 32))).repeat(32)
    a = np.empty((k // 512, 16))
    for p in range(k // 512):
        a[p, :8] = np.random.permutation(np.resize(levels, 8))
        for g in range(8):
            far = levels[np.abs(levels - a[p, g]) >= 10]
            a[p, g + 8] = far[np.random.randint(len(far))]
    return np.exp2(a.ravel()).repeat(32)


def f64(x):
    return np.asarray(x).astype(np.float64)


def striped(idx):
    return np.tile(idx.reshape(-1, 16).T, (8, 1)).astype(np.uint16)


def unstriped(offs):
    return offs[:16].T.reshape(-1).astype(np.int64)


def striped8(idx):
    return np.concatenate([x.reshape(-1, 16).T for x in idx]).astype(np.uint16)


def runs(offs, k):
    lists = np.stack([offs[16 * r : 16 * r + 16].T.reshape(-1) for r in range(8)]).astype(np.int64)
    return lists[np.arange(k) % 512 // 64]


def pack_weight(w):
    k, n = w.shape
    w = f64(np.asarray(w, np.float32).astype(ml_dtypes.bfloat16)).reshape(k // 32, 32, n)
    amax = np.abs(w).max(1)
    byte = np.clip(np.where(amax > 0, np.frexp(amax)[1] - 1 + 127 - 7, 1), 1, 254)
    scaled = (w * np.exp2(127.0 - byte)[:, None, :]).reshape(k, n).astype(np.float32)
    words = np.ascontiguousarray(scaled.reshape(k // 512, 128, 4, n).transpose(0, 1, 3, 2)).astype(ml_dtypes.float8_e4m3fn).view(np.uint8)
    return words, np.ascontiguousarray(byte.astype(np.uint8).reshape(k // 512, 16, n))


def unpack_weight(words, scales):
    g, p, n, _ = words.shape
    vals = np.ascontiguousarray(words).view(ml_dtypes.float8_e4m3fn).astype(np.float64) * np.repeat(np.exp2(scales.astype(np.float64) - 127.0), 8, axis=1)[..., None]
    return vals.transpose(0, 1, 3, 2).reshape(g * 512, n)


def sigmoid(v):
    return 1.0 / (1.0 + np.exp(-np.maximum(v, -700.0)))


K, T, S, N, H = 512, 2048, 512, 512, 512


def setup_inputs():
    n = np.random.standard_normal
    s = mx_kscale(K)[:, None]
    u = mx_kscale(H)
    packed_xT = pack_weight(n((K, T)) * s)
    return {
        "x_words": packed_xT[0],
        "x_scales": packed_xT[1],
        "w1": (n((K, H)) / np.sqrt(K) / s).astype(np.float32),
        "gn": (np.random.uniform(0.5, 1.5, (H, 1)) * u[:, None]).astype(np.float32),
        "w2": (n((H, N)) / np.sqrt(H) / u[:, None]).astype(np.float32),
        "gm": (np.random.uniform(0.5, 1.5, (H, 1)) * u[:, None]).astype(np.float32),
        "w3": (n((H, N)) / np.sqrt(H) / u[:, None]).astype(np.float32),
        "offs": striped(np.random.permutation(T)[:S]),
        "n1": striped8(np.stack([np.random.permutation(S) for _ in range(8)])),
        "n2": striped8(np.stack([np.random.permutation(S) for _ in range(8)])),
        "n3": striped8(np.stack([np.random.permutation(S) for _ in range(8)])),
        "n4": striped8(np.stack([np.random.permutation(S) for _ in range(8)])),
        "n5": striped8(np.stack([np.random.permutation(S) for _ in range(8)])),
        "n6": striped8(np.stack([np.random.permutation(S) for _ in range(8)])),
        "n7": striped8(np.stack([np.random.permutation(S) for _ in range(8)])),
    }


def reference(x_words, x_scales, w1, gn, w2, gm, w3, offs, n1, n2, n3, n4, n5, n6, n7):
    xq = unpack_weight(x_words, x_scales)[:, unstriped(offs)]
    y = mxq(f64(w1), 0, "e4m3").T @ xq
    z = f64(gn) * ((y * (y[np.arange(H)[:, None], runs(n1, H)])) * (np.tanh(y[np.arange(H)[:, None], runs(n2, H)])))
    a = mxq(f64(w2), 0, "e4m3").T @ mxq(z, 0, "e4m3")
    st = y[np.arange(H)[:, None], runs(n3, H)] - y
    z2 = f64(gm) * (y * (sigmoid(st[np.arange(H)[:, None], runs(n4, H)])))
    b = mxq(f64(w3), 0, "e4m3").T @ mxq(z2, 0, "e4m3")
    return np.maximum(np.minimum(a - (0.5 * (a[np.arange(N)[:, None], runs(n5, N)])), b[np.arange(N)[:, None], runs(n6, N)]), b[np.arange(N)[:, None], runs(n7, N)])

@@ -1,0 +1,203 @@
+from contextlib import ExitStack
+
+import concourse.mybir as mybir
+
+K, T, S, N, H = 512, 2048, 512, 512, 512
+FLOPS = 2 * S * (K * H + 2 * H * N)
+
+F32 = mybir.dt.float32
+BF16 = mybir.dt.bfloat16
+I32 = mybir.dt.int32
+U32 = mybir.dt.uint32
+U16 = mybir.dt.uint16
+U8 = mybir.dt.uint8
+FP8X4 = mybir.dt.float8_e4m3fn_x4
+ALU = mybir.AluOpType
+ACT = mybir.ActivationFunctionType
+
+P = 128
+PACK = 4
+WINDOW = 2 * S
+
+
+def tile_picked_forkclampbcubehopd_none_p_kernel(tc, x_words, x_scales, w1, gn, w2, gm, w3, offs, n1, n2, n3, n4, n5, n6, n7, out):
+    nc = tc.nc
+    with ExitStack() as ctx:
+        keep = ctx.enter_context(tc.tile_pool(name="keep", bufs=1))
+        psum = ctx.enter_context(tc.psum_pool(name="psum", bufs=1))
+
+        def load_list(name, src):
+            tile = keep.tile([P, S // 16], U16, name=name)
+            nc.sync.dma_start(tile[:], src)
+            return tile
+
+        def load_weight(name, w, pieces):
+            width = 512 // pieces
+            raws = []
+            for h in range(pieces):
+                raw = keep.tile([P, PACK, width], F32, name=f"{name}_raw{h}")
+                nc.sync.dma_start(raw[:], w.rearrange("(p j) c -> p j c", j=PACK)[:, :, h * width : (h + 1) * width])
+                raws.append(raw)
+            return raws
+
+        def deal_weight(name, raws, copies, tag):
+            dealt = keep.tile([P, PACK, P, PACK], BF16, name=f"{name}_dealt", tag=tag, align_bytes=64)
+            span = P // len(raws)
+            for h, raw in enumerate(raws):
+                copies[h](
+                    dealt[:, :, h * span : (h + 1) * span, :].rearrange("p t m j -> p m j t"),
+                    raw[:].rearrange("p j (m t) -> p m j t", t=PACK),
+                )
+            return dealt
+
+        def quantize(name, flat, pieces):
+            codes = keep.tile([P, 512], U32, name=f"{name}_codes", align_bytes=64)
+            scales = keep.tile([P, 512], U8, name=f"{name}_scales", align_bytes=64)
+            width = 512 // pieces
+            for h in range(pieces):
+                cols = slice(h * width, (h + 1) * width)
+                nc.vector.quantize_mx(
+                    out=codes[:, cols].bitcast(FP8X4),
+                    scales=scales[:, cols],
+                    in_=flat[:, PACK * h * width : PACK * (h + 1) * width],
+                )
+            return codes, scales
+
+        def product(bank, t, weight, moving, places=slice(0, S)):
+            acc = psum.tile([P, places.stop - places.start], F32, name=f"bank{bank}", tag=f"bank{bank}")
+            cols = slice(t * P, (t + 1) * P)
+            nc.tensor.matmul_mx(
+                out=acc[:],
+                lhsT=weight[0][:, cols].bitcast(FP8X4),
+                lhsT_scale=weight[1][:, cols],
+                rhs=moving[0][:, places].bitcast(FP8X4),
+                rhs_scale=moving[1][:, places],
+                start=True,
+                stop=True,
+            )
+            return acc
+
+        def windows(name):
+            return [keep.tile([P, WINDOW], F32, name=f"{name}{t}") for t in range(PACK)]
+
+        def planes(name):
+            return keep.tile([P, PACK, S], F32, name=name)
+
+        def weave(name, left, right):
+            woven = keep.tile([P, S, PACK], BF16, name=name, tag=name, align_bytes=64)
+            nc.vector.tensor_tensor(
+                woven[:].rearrange("p (c i) t -> p c t i", i=4),
+                left[:].rearrange("p t (c i) -> p c t i", i=4),
+                right[:].rearrange("p t (c i) -> p c t i", i=4),
+                ALU.mult,
+            )
+            return woven[:].rearrange("p s t -> p (s t)")
+
+        x_scale_table = keep.tile([P, T], U8, name="x_scale_table", align_bytes=64)
+        nc.vector.memset(x_scale_table[:].bitcast(I32), 0)
+        warm = keep.tile([P, 2], F32, name="warm")
+        nc.gpsimd.memset(warm[:, 0:1], 0.0)
+        nc.scalar.activation(warm[:, 1:2], warm[:, 0:1], ACT.Sigmoid)
+        offs_sb = load_list("offs_sb", offs)
+        for q in range(4):
+            nc.sync.dma_start(
+                x_scale_table[32 * q : 32 * q + 4, :].bitcast(I32), x_scales[0, 4 * q : 4 * q + 4, :].bitcast(I32)
+            )
+        w1_raw = load_weight("w1", w1, 2)
+        x_word_table = keep.tile([P, T], U32, name="x_word_table", align_bytes=64)
+        nc.sync.dma_start(x_word_table[:].bitcast(I32), x_words[0].rearrange("p n t -> p (n t)").bitcast(I32))
+        n3_sb = load_list("n3_sb", n3)
+        n1_sb = load_list("n1_sb", n1)
+        n4_sb = load_list("n4_sb", n4)
+        gm_sb = keep.tile([P, PACK], F32, name="gm_sb")
+        nc.sync.dma_start(gm_sb[:], gm.rearrange("(p t) o -> p (t o)", t=PACK))
+        w3_raw = load_weight("w3", w3, 1)
+        gn_sb = keep.tile([P, PACK], F32, name="gn_sb")
+        nc.sync.dma_start(gn_sb[:], gn.rearrange("(p t) o -> p (t o)", t=PACK))
+        n2_sb = load_list("n2_sb", n2)
+        w2_raw = load_weight("w2", w2, 1)
+        n6_sb = load_list("n6_sb", n6)
+        n7_sb = load_list("n7_sb", n7)
+        n5_sb = load_list("n5_sb", n5)
+
+        x_scale = keep.tile([P, S], U8, name="x_scale", align_bytes=64)
+        nc.vector.tensor_copy(x_scale[:], x_scale_table[:].indirect(offs_sb[:]))
+        w1_dealt = deal_weight("w1", w1_raw, [nc.scalar.copy, nc.vector.tensor_copy], "w1_dealt")
+        w1_q = quantize("w1", w1_dealt[:].rearrange("p t m j -> p (t m j)"), 1)
+        x_word = keep.tile([P, S], U32, name="x_word", align_bytes=64)
+        halves = [slice(0, S // 2), slice(S // 2, S)]
+        for half in halves:
+            nc.vector.tensor_copy(
+                x_word[:, half], x_word_table[:].indirect(offs_sb[:, half.start // 16 : half.stop // 16])
+            )
+
+        y_win = windows("y_win")
+        st_win = windows("st_win")
+        y_plain = planes("y_plain")
+        y_parts = []
+        for t in range(PACK):
+            parts = []
+            for places in halves if t == 0 else [slice(0, S)]:
+                acc = product(len(parts) * PACK + t, t, w1_q, (x_word, x_scale), places)
+                parts.append((places, acc))
+                nc.scalar.copy(y_win[t][:, places], acc[:])
+                nc.scalar.copy(y_plain[:, t, places], acc[:])
+            y_parts.append(parts)
+            nc.vector.tensor_tensor(st_win[t][:, 0:S], y_win[t][:].indirect(n3_sb[:]), y_plain[:, t, :], ALU.subtract)
+
+        gate = planes("gate")
+        y_gm = planes("y_gm")
+        for t in range(PACK):
+            nc.scalar.activation(gate[:, t, :], st_win[t][:].indirect(n4_sb[:]), ACT.Sigmoid)
+            for places, acc in y_parts[t]:
+                nc.scalar.activation(y_gm[:, t, places], acc[:], ACT.Copy, scale=gm_sb[:, t : t + 1])
+        pair = planes("pair")
+        for t in range(PACK):
+            nc.vector.tensor_tensor(pair[:, t, :], y_win[t][:].indirect(n1_sb[:]), y_plain[:, t, :], ALU.mult)
+        w3_dealt = deal_weight("w3", w3_raw, [nc.vector.tensor_copy], "w3_dealt")
+        w3_q = quantize("w3", w3_dealt[:].rearrange("p t m j -> p (t m j)"), 1)
+        z2_q = quantize("z2", weave("z2", gate, y_gm), 1)
+        w2_dealt = deal_weight("w2", w2_raw, [nc.vector.tensor_copy], "z2")
+        w2_q = quantize("w2", w2_dealt[:].rearrange("p t m j -> p (t m j)"), 1)
+
+        b_win = windows("b_win")
+        cap = planes("cap")
+        for t in range(PACK):
+            acc = product(PACK + t, t, w3_q, z2_q)
+            nc.scalar.copy(b_win[t][:, 0:S], acc[:])
+
+        gn_twice = keep.tile([P, PACK], F32, name="gn_twice")
+        nc.gpsimd.tensor_scalar(gn_twice[:], gn_sb[:], 2.0, 0.0, ALU.mult, ALU.add)
+        gn_minus = keep.tile([P, PACK], F32, name="gn_minus")
+        nc.gpsimd.tensor_scalar(gn_minus[:], gn_sb[:], -1.0, 0.0, ALU.mult, ALU.add)
+        sig = planes("sig")
+        tanh_gn = planes("tanh_gn")
+        for t in range(PACK):
+            nc.scalar.activation(sig[:, t, :], y_win[t][:].indirect(n2_sb[:]), ACT.Sigmoid, scale=2.0)
+            nc.scalar.activation(
+                tanh_gn[:, t, :], sig[:, t, :], ACT.Identity, scale=gn_twice[:, t : t + 1], bias=gn_minus[:, t : t + 1]
+            )
+        for t in range(PACK):
+            nc.vector.tensor_copy(cap[:, t, :], b_win[t][:].indirect(n6_sb[:]))
+        z_q = quantize("z", weave("z", pair, tanh_gn), 1)
+        low_early = keep.tile([P, 2, S], F32, name="low_early")
+        low_late = keep.tile([P, 2, S], F32, name="low_late", tag="z", align_bytes=64)
+        low = [low_early[:, 0, :], low_early[:, 1, :], low_late[:, 0, :], low_late[:, 1, :]]
+        for t in range(PACK):
+            nc.vector.tensor_copy(low[t], b_win[t][:].indirect(n7_sb[:]))
+
+        a_win = windows("a_win")
+        a_plain = planes("a_plain")
+        diff = planes("diff")
+        capped = planes("capped")
+        result = planes("result")
+        out_rows = out.rearrange("(p t) s -> p t s", t=PACK)
+        for t in range(PACK):
+            acc = product(t, t, w2_q, z_q)
+            nc.scalar.activation(a_win[t][:, 0:S], acc[:], ACT.Copy, scale=-0.5)
+            nc.scalar.copy(a_plain[:, t, :], acc[:])
+        for t in range(PACK):
+            nc.vector.tensor_tensor(diff[:, t, :], a_win[t][:].indirect(n5_sb[:]), a_plain[:, t, :], ALU.add)
+            nc.vector.tensor_tensor(capped[:, t, :], diff[:, t, :], cap[:, t, :], ALU.min)
+            nc.vector.tensor_tensor(result[:, t, :], capped[:, t, :], low[t], ALU.max)
+            nc.sync.dma_start(out_rows[:, t, :], result[:, t, :])

@@ -35,7 +35,7 @@ def tile_picked_forkclampbcubehopd_none_p_kernel(tc, x_words, x_scales, w1, gn, 
             width = 512 // pieces
             raws = []
             for h in range(pieces):
-                raw = keep.tile([P, PACK, width], F32, name=f"{name}_raw{h}")
+                raw = keep.tile([P, PACK, width], F32, name=f"{name}_raw{h}", tag=f"{name}_raw{h}")
                 nc.sync.dma_start(raw[:], w.rearrange("(p j) c -> p j c", j=PACK)[:, :, h * width : (h + 1) * width])
                 raws.append(raw)
             return raws
@@ -48,19 +48,15 @@ def tile_picked_forkclampbcubehopd_none_p_kernel(tc, x_words, x_scales, w1, gn, 
                     dealt[:, :, h * span : (h + 1) * span, :].rearrange("p t m j -> p m j t"),
                     raw[:].rearrange("p j (m t) -> p m j t", t=PACK),
                 )
-            return dealt
+            return [dealt[:].rearrange("p t m j -> p (t m j)")]
 
-        def quantize(name, flat, pieces):
-            codes = keep.tile([P, 512], U32, name=f"{name}_codes", align_bytes=64)
+        def quantize(name, pieces):
+            codes = keep.tile([P, 512], U32, name=f"{name}_codes", tag=f"{name}_codes", align_bytes=64)
             scales = keep.tile([P, 512], U8, name=f"{name}_scales", align_bytes=64)
-            width = 512 // pieces
-            for h in range(pieces):
+            width = 512 // len(pieces)
+            for h, piece in enumerate(pieces):
                 cols = slice(h * width, (h + 1) * width)
-                nc.vector.quantize_mx(
-                    out=codes[:, cols].bitcast(FP8X4),
-                    scales=scales[:, cols],
-                    in_=flat[:, PACK * h * width : PACK * (h + 1) * width],
-                )
+                nc.vector.quantize_mx(out=codes[:, cols].bitcast(FP8X4), scales=scales[:, cols], in_=piece)
             return codes, scales
 
         def product(bank, t, weight, moving, places=slice(0, S)):
@@ -78,25 +74,30 @@ def tile_picked_forkclampbcubehopd_none_p_kernel(tc, x_words, x_scales, w1, gn, 
             return acc
 
         def windows(name):
-            return [keep.tile([P, WINDOW], F32, name=f"{name}{t}") for t in range(PACK)]
+            return [keep.tile([P, WINDOW], F32, name=f"{name}{t}", tag=f"{name}{t}", align_bytes=64) for t in range(PACK)]
 
         def planes(name):
             return keep.tile([P, PACK, S], F32, name=name)
 
-        def weave(name, left, right):
-            woven = keep.tile([P, S, PACK], BF16, name=name, tag=name, align_bytes=64)
-            nc.vector.tensor_tensor(
-                woven[:].rearrange("p (c i) t -> p c t i", i=4),
-                left[:].rearrange("p t (c i) -> p c t i", i=4),
-                right[:].rearrange("p t (c i) -> p c t i", i=4),
-                ALU.mult,
-            )
-            return woven[:].rearrange("p s t -> p (s t)")
+        halves = [slice(0, S // 2), slice(S // 2, S)]
 
-        x_scale_table = keep.tile([P, T], U8, name="x_scale_table", align_bytes=64)
-        nc.vector.memset(x_scale_table[:].bitcast(I32), 0)
+        def weave(room, left, right):
+            pieces = []
+            for h, half in enumerate(halves):
+                woven = room[:, h * S : (h + 1) * S].bitcast(BF16)
+                nc.vector.tensor_tensor(
+                    woven.rearrange("p (c i t) -> p c t i", i=4, t=PACK),
+                    left[:, :, half].rearrange("p t (c i) -> p c t i", i=4),
+                    right[:, :, half].rearrange("p t (c i) -> p c t i", i=4),
+                    ALU.mult,
+                )
+                pieces.append(woven)
+            return pieces
+
         warm = keep.tile([P, 2], F32, name="warm")
         nc.gpsimd.memset(warm[:, 0:1], 0.0)
+        x_scale_table = keep.tile([P, T], U8, name="x_scale_table", align_bytes=64)
+        nc.gpsimd.memset(x_scale_table[:].bitcast(I32), 0)
         nc.scalar.activation(warm[:, 1:2], warm[:, 0:1], ACT.Sigmoid)
         offs_sb = load_list("offs_sb", offs)
         for q in range(4):
@@ -122,10 +123,8 @@ def tile_picked_forkclampbcubehopd_none_p_kernel(tc, x_words, x_scales, w1, gn, 
 
         x_scale = keep.tile([P, S], U8, name="x_scale", align_bytes=64)
         nc.vector.tensor_copy(x_scale[:], x_scale_table[:].indirect(offs_sb[:]))
-        w1_dealt = deal_weight("w1", w1_raw, [nc.scalar.copy, nc.vector.tensor_copy], "w1_dealt")
-        w1_q = quantize("w1", w1_dealt[:].rearrange("p t m j -> p (t m j)"), 1)
+        w1_q = quantize("w1", deal_weight("w1", w1_raw, [nc.scalar.copy, nc.vector.tensor_copy], "w1_dealt"))
         x_word = keep.tile([P, S], U32, name="x_word", align_bytes=64)
-        halves = [slice(0, S // 2), slice(S // 2, S)]
         for half in halves:
             nc.vector.tensor_copy(
                 x_word[:, half], x_word_table[:].indirect(offs_sb[:, half.start // 16 : half.stop // 16])
@@ -134,34 +133,33 @@ def tile_picked_forkclampbcubehopd_none_p_kernel(tc, x_words, x_scales, w1, gn, 
         y_win = windows("y_win")
         st_win = windows("st_win")
         y_plain = planes("y_plain")
-        y_parts = []
         for t in range(PACK):
-            parts = []
-            for places in halves if t == 0 else [slice(0, S)]:
-                acc = product(len(parts) * PACK + t, t, w1_q, (x_word, x_scale), places)
-                parts.append((places, acc))
+            for part, places in enumerate(halves if t == 0 else [slice(0, S)]):
+                acc = product(part * PACK + t, t, w1_q, (x_word, x_scale), places)
                 nc.scalar.copy(y_win[t][:, places], acc[:])
                 nc.scalar.copy(y_plain[:, t, places], acc[:])
-            y_parts.append(parts)
             nc.vector.tensor_tensor(st_win[t][:, 0:S], y_win[t][:].indirect(n3_sb[:]), y_plain[:, t, :], ALU.subtract)
 
         gate = planes("gate")
-        y_gm = planes("y_gm")
         for t in range(PACK):
             nc.scalar.activation(gate[:, t, :], st_win[t][:].indirect(n4_sb[:]), ACT.Sigmoid)
-            for places, acc in y_parts[t]:
-                nc.scalar.activation(y_gm[:, t, places], acc[:], ACT.Copy, scale=gm_sb[:, t : t + 1])
-        pair = planes("pair")
-        for t in range(PACK):
+        pair_room = keep.tile([P, (PACK + 1) * S], F32, name="pair_room", align_bytes=64)
+        pair = pair_room[:, 0 : PACK * S].rearrange("p (t s) -> p t s", t=PACK)
+
+        def pair_product(t):
             nc.vector.tensor_tensor(pair[:, t, :], y_win[t][:].indirect(n1_sb[:]), y_plain[:, t, :], ALU.mult)
-        w3_dealt = deal_weight("w3", w3_raw, [nc.vector.tensor_copy], "w3_dealt")
-        w3_q = quantize("w3", w3_dealt[:].rearrange("p t m j -> p (t m j)"), 1)
-        z2_q = quantize("z2", weave("z2", gate, y_gm), 1)
-        w2_dealt = deal_weight("w2", w2_raw, [nc.vector.tensor_copy], "z2")
-        w2_q = quantize("w2", w2_dealt[:].rearrange("p t m j -> p (t m j)"), 1)
+
+        for t in range(PACK - 1):
+            pair_product(t)
+        y_gm = planes("y_gm")
+        for t in range(PACK):
+            nc.vector.tensor_scalar(y_gm[:, t, :], y_plain[:, t, :], gm_sb[:, t : t + 1], None, ALU.mult)
+        w3_dealt = deal_weight("w3", w3_raw, [nc.scalar.copy], "st_win2")
+        z2_q = quantize("z2", weave(pair_room[:, (PACK - 1) * S :], gate, y_gm))
+        w3_q = quantize("w3", w3_dealt)
+        pair_product(PACK - 1)
 
         b_win = windows("b_win")
-        cap = planes("cap")
         for t in range(PACK):
             acc = product(PACK + t, t, w3_q, z2_q)
             nc.scalar.copy(b_win[t][:, 0:S], acc[:])
@@ -170,34 +168,46 @@ def tile_picked_forkclampbcubehopd_none_p_kernel(tc, x_words, x_scales, w1, gn, 
         nc.gpsimd.tensor_scalar(gn_twice[:], gn_sb[:], 2.0, 0.0, ALU.mult, ALU.add)
         gn_minus = keep.tile([P, PACK], F32, name="gn_minus")
         nc.gpsimd.tensor_scalar(gn_minus[:], gn_sb[:], -1.0, 0.0, ALU.mult, ALU.add)
-        sig = planes("sig")
+        sig_first = keep.tile([P, S], F32, name="sig_first")
+        sig_rest = keep.tile([P, PACK - 1, S], F32, name="sig_rest", tag="z2_codes", align_bytes=64)
+        sig = [sig_first[:]] + [sig_rest[:, t, :] for t in range(PACK - 1)]
         tanh_gn = planes("tanh_gn")
         for t in range(PACK):
-            nc.scalar.activation(sig[:, t, :], y_win[t][:].indirect(n2_sb[:]), ACT.Sigmoid, scale=2.0)
+            nc.scalar.activation(sig[t], y_win[t][:].indirect(n2_sb[:]), ACT.Sigmoid, scale=2.0)
             nc.scalar.activation(
-                tanh_gn[:, t, :], sig[:, t, :], ACT.Identity, scale=gn_twice[:, t : t + 1], bias=gn_minus[:, t : t + 1]
+                tanh_gn[:, t, :], sig[t], ACT.Identity, scale=gn_twice[:, t : t + 1], bias=gn_minus[:, t : t + 1]
             )
+        w2_dealt = deal_weight("w2", w2_raw, [nc.scalar.copy], "z2_codes")
+        cap = planes("cap")
         for t in range(PACK):
             nc.vector.tensor_copy(cap[:, t, :], b_win[t][:].indirect(n6_sb[:]))
-        z_q = quantize("z", weave("z", pair, tanh_gn), 1)
-        low_early = keep.tile([P, 2, S], F32, name="low_early")
-        low_late = keep.tile([P, 2, S], F32, name="low_late", tag="z", align_bytes=64)
-        low = [low_early[:, 0, :], low_early[:, 1, :], low_late[:, 0, :], low_late[:, 1, :]]
+        low_room = keep.tile([P, PACK * S], F32, name="low_room", align_bytes=64)
+        low = [low_room[:, t * S : (t + 1) * S] for t in range(PACK)]
+        z_q = quantize("z", weave(low_room[:, 2 * S :], pair, tanh_gn))
+        w2_q = quantize("w2", w2_dealt)
         for t in range(PACK):
             nc.vector.tensor_copy(low[t], b_win[t][:].indirect(n7_sb[:]))
 
         a_win = windows("a_win")
         a_plain = planes("a_plain")
-        diff = planes("diff")
-        capped = planes("capped")
-        result = planes("result")
         out_rows = out.rearrange("(p t) s -> p t s", t=PACK)
         for t in range(PACK):
             acc = product(t, t, w2_q, z_q)
             nc.scalar.activation(a_win[t][:, 0:S], acc[:], ACT.Copy, scale=-0.5)
             nc.scalar.copy(a_plain[:, t, :], acc[:])
-        for t in range(PACK):
+        diff = keep.tile([P, PACK, S], F32, name="diff", tag="z_codes", align_bytes=64)
+
+        def hop(t):
             nc.vector.tensor_tensor(diff[:, t, :], a_win[t][:].indirect(n5_sb[:]), a_plain[:, t, :], ALU.add)
-            nc.vector.tensor_tensor(capped[:, t, :], diff[:, t, :], cap[:, t, :], ALU.min)
-            nc.vector.tensor_tensor(result[:, t, :], capped[:, t, :], low[t], ALU.max)
-            nc.sync.dma_start(out_rows[:, t, :], result[:, t, :])
+
+        def smaller(t):
+            nc.vector.tensor_tensor(diff[:, t, :], diff[:, t, :], cap[:, t, :], ALU.min)
+
+        def larger(t):
+            nc.vector.tensor_tensor(diff[:, t, :], diff[:, t, :], low[t], ALU.max)
+            nc.sync.dma_start(out_rows[:, t, :], diff[:, t, :])
+
+        for step in range(PACK + 2):
+            for stage, lag in ((hop, 0), (smaller, 1), (larger, 2)):
+                if 0 <= step - lag < PACK:
+                    stage(step - lag)

@@ -81,18 +81,15 @@ def tile_picked_forkclampbcubehopd_none_p_kernel(tc, x_words, x_scales, w1, gn, 
 
         halves = [slice(0, S // 2), slice(S // 2, S)]
 
-        def weave(room, left, right):
-            pieces = []
-            for h, half in enumerate(halves):
-                woven = room[:, h * S : (h + 1) * S].bitcast(BF16)
-                nc.vector.tensor_tensor(
-                    woven.rearrange("p (c i t) -> p c t i", i=4, t=PACK),
-                    left[:, :, half].rearrange("p t (c i) -> p c t i", i=4),
-                    right[:, :, half].rearrange("p t (c i) -> p c t i", i=4),
-                    ALU.mult,
-                )
-                pieces.append(woven)
-            return pieces
+        def weave(engine, room, h, left, right):
+            woven = room[:, h * S : (h + 1) * S].bitcast(BF16)
+            engine.tensor_tensor(
+                woven.rearrange("p (c i t) -> p c t i", i=4, t=PACK),
+                left[:, :, halves[h]].rearrange("p t (c i) -> p c t i", i=4),
+                right[:, :, halves[h]].rearrange("p t (c i) -> p c t i", i=4),
+                ALU.mult,
+            )
+            return woven
 
         warm = keep.tile([P, 2], F32, name="warm")
         nc.gpsimd.memset(warm[:, 0:1], 0.0)
@@ -132,7 +129,7 @@ def tile_picked_forkclampbcubehopd_none_p_kernel(tc, x_words, x_scales, w1, gn, 
 
         y_win = windows("y_win")
         st_win = windows("st_win")
-        y_plain = planes("y_plain")
+        y_plain = keep.tile([P, PACK, S], F32, name="y_plain", tag="y_plain")
         for t in range(PACK):
             for part, places in enumerate(halves if t == 0 else [slice(0, S)]):
                 acc = product(part * PACK + t, t, w1_q, (x_word, x_scale), places)
@@ -155,7 +152,7 @@ def tile_picked_forkclampbcubehopd_none_p_kernel(tc, x_words, x_scales, w1, gn, 
         for t in range(PACK):
             nc.vector.tensor_scalar(y_gm[:, t, :], y_plain[:, t, :], gm_sb[:, t : t + 1], None, ALU.mult)
         w3_dealt = deal_weight("w3", w3_raw, [nc.scalar.copy], "st_win2")
-        z2_q = quantize("z2", weave(pair_room[:, (PACK - 1) * S :], gate, y_gm))
+        z2_q = quantize("z2", [weave(nc.vector, pair_room[:, (PACK - 1) * S :], h, gate, y_gm) for h in range(2)])
         w3_q = quantize("w3", w3_dealt)
         pair_product(PACK - 1)
 
@@ -168,23 +165,27 @@ def tile_picked_forkclampbcubehopd_none_p_kernel(tc, x_words, x_scales, w1, gn, 
         nc.gpsimd.tensor_scalar(gn_twice[:], gn_sb[:], 2.0, 0.0, ALU.mult, ALU.add)
         gn_minus = keep.tile([P, PACK], F32, name="gn_minus")
         nc.gpsimd.tensor_scalar(gn_minus[:], gn_sb[:], -1.0, 0.0, ALU.mult, ALU.add)
-        sig_first = keep.tile([P, S], F32, name="sig_first")
-        sig_rest = keep.tile([P, PACK - 1, S], F32, name="sig_rest", tag="z2_codes", align_bytes=64)
-        sig = [sig_first[:]] + [sig_rest[:, t, :] for t in range(PACK - 1)]
-        tanh_gn = planes("tanh_gn")
-        for t in range(PACK):
-            nc.scalar.activation(sig[t], y_win[t][:].indirect(n2_sb[:]), ACT.Sigmoid, scale=2.0)
-            nc.scalar.activation(
-                tanh_gn[:, t, :], sig[t], ACT.Identity, scale=gn_twice[:, t : t + 1], bias=gn_minus[:, t : t + 1]
-            )
-        w2_dealt = deal_weight("w2", w2_raw, [nc.scalar.copy], "z2_codes")
+        sig = [
+            keep.tile([P, PACK, S // 2], F32, name="sig0"),
+            keep.tile([P, PACK, S // 2], F32, name="sig1", tag="z2_codes", align_bytes=64),
+        ]
+        tanh_gn = keep.tile([P, PACK, S], F32, name="tanh_gn", tag="y_plain")
+        low_room = keep.tile([P, PACK * S], F32, name="low_room", align_bytes=64)
+        low = [low_room[:, t * S : (t + 1) * S] for t in range(PACK)]
+        for h, half in enumerate(halves):
+            for t in range(PACK):
+                entries = n2_sb[:, half.start // 16 : half.stop // 16]
+                nc.scalar.activation(sig[h][:, t, :], y_win[t][:].indirect(entries), ACT.Sigmoid, scale=2.0)
+                nc.gpsimd.tensor_scalar(
+                    tanh_gn[:, t, half], sig[h][:, t, :], gn_twice[:, t : t + 1], gn_minus[:, t : t + 1], ALU.mult, ALU.add
+                )
+            weave(nc.gpsimd, low_room[:, 2 * S :], h, pair, tanh_gn)
+        w2_dealt = deal_weight("w2", w2_raw, [nc.scalar.copy], "y_win2")
         cap = planes("cap")
         for t in range(PACK):
             nc.vector.tensor_copy(cap[:, t, :], b_win[t][:].indirect(n6_sb[:]))
-        low_room = keep.tile([P, PACK * S], F32, name="low_room", align_bytes=64)
-        low = [low_room[:, t * S : (t + 1) * S] for t in range(PACK)]
-        z_q = quantize("z", weave(low_room[:, 2 * S :], pair, tanh_gn))
         w2_q = quantize("w2", w2_dealt)
+        z_q = quantize("z", [low_room[:, 2 * S :].bitcast(BF16)])
         for t in range(PACK):
             nc.vector.tensor_copy(low[t], b_win[t][:].indirect(n7_sb[:]))
 

@@ -17,25 +17,44 @@ ACT = mybir.ActivationFunctionType
 
 P = 128
 PACK = 4
+LAST = PACK - 1
+WIDTH = 512
+GROUP = 16
+QUADRANT = 32
 WINDOW = 2 * S
+RUN = 4
+ALL = slice(0, S)
+HALVES = (slice(0, S // 2), slice(S // 2, S))
+THIRD_QUARTER = slice(S // 2, 3 * S // 4)
+LAST_QUARTER = slice(3 * S // 4, S)
 
 
-def tile_picked_forkclampbcubehopd_none_p_kernel(tc, x_words, x_scales, w1, gn, w2, gm, w3, offs, n1, n2, n3, n4, n5, n6, n7, out):
+def tile_picked_forkclampbcubehopd_none_p_kernel(
+    tc, x_words, x_scales, w1, gn, w2, gm, w3, offs, n1, n2, n3, n4, n5, n6, n7, out
+):
     nc = tc.nc
     with ExitStack() as ctx:
         keep = ctx.enter_context(tc.tile_pool(name="keep", bufs=1))
         psum = ctx.enter_context(tc.psum_pool(name="psum", bufs=1))
 
         def load_list(name, src):
-            tile = keep.tile([P, S // 16], U16, name=name)
-            nc.sync.dma_start(tile[:], src)
-            return tile
+            entries = keep.tile([P, S // GROUP], U16, name=name)
+            nc.sync.dma_start(entries[:], src)
+            return entries
+
+        def entries_for(entries, places):
+            return entries[:, places.start // GROUP : places.stop // GROUP]
+
+        def load_gain(name, gain):
+            per_plane = keep.tile([P, PACK], F32, name=name)
+            nc.sync.dma_start(per_plane[:], gain.rearrange("(p t) o -> p (t o)", t=PACK))
+            return per_plane
 
         def load_weight(name, w, pieces):
-            width = 512 // pieces
+            width = WIDTH // pieces
             raws = []
             for h in range(pieces):
-                raw = keep.tile([P, PACK, width], F32, name=f"{name}_raw{h}", tag=f"{name}_raw{h}")
+                raw = keep.tile([P, PACK, width], F32, name=f"{name}_raw{h}")
                 nc.sync.dma_start(raw[:], w.rearrange("(p j) c -> p j c", j=PACK)[:, :, h * width : (h + 1) * width])
                 raws.append(raw)
             return raws
@@ -48,18 +67,18 @@ def tile_picked_forkclampbcubehopd_none_p_kernel(tc, x_words, x_scales, w1, gn, 
                     dealt[:, :, h * span : (h + 1) * span, :].rearrange("p t m j -> p m j t"),
                     raw[:].rearrange("p j (m t) -> p m j t", t=PACK),
                 )
-            return [dealt[:].rearrange("p t m j -> p (t m j)")]
+            return dealt[:].rearrange("p t m j -> p (t m j)")
 
         def quantize(name, pieces):
-            codes = keep.tile([P, 512], U32, name=f"{name}_codes", tag=f"{name}_codes", align_bytes=64)
-            scales = keep.tile([P, 512], U8, name=f"{name}_scales", align_bytes=64)
-            width = 512 // len(pieces)
+            codes = keep.tile([P, WIDTH], U32, name=f"{name}_codes", tag=f"{name}_codes", align_bytes=64)
+            scales = keep.tile([P, WIDTH], U8, name=f"{name}_scales", align_bytes=64)
+            width = WIDTH // len(pieces)
             for h, piece in enumerate(pieces):
                 cols = slice(h * width, (h + 1) * width)
                 nc.vector.quantize_mx(out=codes[:, cols].bitcast(FP8X4), scales=scales[:, cols], in_=piece)
             return codes, scales
 
-        def product(bank, t, weight, moving, places=slice(0, S)):
+        def product(bank, t, weight, moving, places):
             acc = psum.tile([P, places.stop - places.start], F32, name=f"bank{bank}", tag=f"bank{bank}")
             cols = slice(t * P, (t + 1) * P)
             nc.tensor.matmul_mx(
@@ -76,30 +95,23 @@ def tile_picked_forkclampbcubehopd_none_p_kernel(tc, x_words, x_scales, w1, gn, 
         def windows(name):
             return [keep.tile([P, WINDOW], F32, name=f"{name}{t}", tag=f"{name}{t}", align_bytes=64) for t in range(PACK)]
 
-        def planes(name):
-            return keep.tile([P, PACK, S], F32, name=name)
-
-        halves = [slice(0, S // 2), slice(S // 2, S)]
-
-        def weave(engine, room, h, left, right):
-            woven = room[:, h * S : (h + 1) * S].bitcast(BF16)
+        def weave(engine, room, places, left, right):
+            woven = room.bitcast(BF16)[:, PACK * places.start : PACK * places.stop]
             engine.tensor_tensor(
-                woven.rearrange("p (c i t) -> p c t i", i=4, t=PACK),
-                left[:, :, halves[h]].rearrange("p t (c i) -> p c t i", i=4),
-                right[:, :, halves[h]].rearrange("p t (c i) -> p c t i", i=4),
+                woven.rearrange("p (c i t) -> p c t i", i=RUN, t=PACK),
+                left[:, :, places].rearrange("p t (c i) -> p c t i", i=RUN),
+                right[:, :, places].rearrange("p t (c i) -> p c t i", i=RUN),
                 ALU.mult,
             )
             return woven
 
-        warm = keep.tile([P, 2], F32, name="warm")
-        nc.gpsimd.memset(warm[:, 0:1], 0.0)
         x_scale_table = keep.tile([P, T], U8, name="x_scale_table", align_bytes=64)
         nc.gpsimd.memset(x_scale_table[:].bitcast(I32), 0)
-        nc.scalar.activation(warm[:, 1:2], warm[:, 0:1], ACT.Sigmoid)
         offs_sb = load_list("offs_sb", offs)
-        for q in range(4):
+        for q in range(P // QUADRANT):
             nc.sync.dma_start(
-                x_scale_table[32 * q : 32 * q + 4, :].bitcast(I32), x_scales[0, 4 * q : 4 * q + 4, :].bitcast(I32)
+                x_scale_table[QUADRANT * q : QUADRANT * q + PACK, :].bitcast(I32),
+                x_scales[0, PACK * q : PACK * (q + 1), :].bitcast(I32),
             )
         w1_raw = load_weight("w1", w1, 2)
         x_word_table = keep.tile([P, T], U32, name="x_word_table", align_bytes=64)
@@ -107,11 +119,9 @@ def tile_picked_forkclampbcubehopd_none_p_kernel(tc, x_words, x_scales, w1, gn, 
         n3_sb = load_list("n3_sb", n3)
         n1_sb = load_list("n1_sb", n1)
         n4_sb = load_list("n4_sb", n4)
-        gm_sb = keep.tile([P, PACK], F32, name="gm_sb")
-        nc.sync.dma_start(gm_sb[:], gm.rearrange("(p t) o -> p (t o)", t=PACK))
+        gm_sb = load_gain("gm_sb", gm)
         w3_raw = load_weight("w3", w3, 1)
-        gn_sb = keep.tile([P, PACK], F32, name="gn_sb")
-        nc.sync.dma_start(gn_sb[:], gn.rearrange("(p t) o -> p (t o)", t=PACK))
+        gn_sb = load_gain("gn_sb", gn)
         n2_sb = load_list("n2_sb", n2)
         w2_raw = load_weight("w2", w2, 1)
         n6_sb = load_list("n6_sb", n6)
@@ -120,46 +130,46 @@ def tile_picked_forkclampbcubehopd_none_p_kernel(tc, x_words, x_scales, w1, gn, 
 
         x_scale = keep.tile([P, S], U8, name="x_scale", align_bytes=64)
         nc.vector.tensor_copy(x_scale[:], x_scale_table[:].indirect(offs_sb[:]))
-        w1_q = quantize("w1", deal_weight("w1", w1_raw, [nc.scalar.copy, nc.vector.tensor_copy], "w1_dealt"))
+        w1_q = quantize("w1", [deal_weight("w1", w1_raw, [nc.scalar.copy, nc.vector.tensor_copy], "w1_dealt")])
         x_word = keep.tile([P, S], U32, name="x_word", align_bytes=64)
-        for half in halves:
-            nc.vector.tensor_copy(
-                x_word[:, half], x_word_table[:].indirect(offs_sb[:, half.start // 16 : half.stop // 16])
-            )
+        for half in HALVES:
+            nc.vector.tensor_copy(x_word[:, half], x_word_table[:].indirect(entries_for(offs_sb, half)))
 
         y_win = windows("y_win")
         st_win = windows("st_win")
         y_plain = keep.tile([P, PACK, S], F32, name="y_plain", tag="y_plain")
         for t in range(PACK):
-            for part, places in enumerate(halves if t == 0 else [slice(0, S)]):
+            for part, places in enumerate(HALVES if t == 0 else [ALL]):
                 acc = product(part * PACK + t, t, w1_q, (x_word, x_scale), places)
                 nc.scalar.copy(y_win[t][:, places], acc[:])
                 nc.scalar.copy(y_plain[:, t, places], acc[:])
-            nc.vector.tensor_tensor(st_win[t][:, 0:S], y_win[t][:].indirect(n3_sb[:]), y_plain[:, t, :], ALU.subtract)
+            nc.vector.tensor_tensor(st_win[t][:, ALL], y_win[t][:].indirect(n3_sb[:]), y_plain[:, t, :], ALU.subtract)
 
-        gate = planes("gate")
+        gate = keep.tile([P, PACK, S], F32, name="gate")
         for t in range(PACK):
             nc.scalar.activation(gate[:, t, :], st_win[t][:].indirect(n4_sb[:]), ACT.Sigmoid)
+
         pair_room = keep.tile([P, (PACK + 1) * S], F32, name="pair_room", align_bytes=64)
         pair = pair_room[:, 0 : PACK * S].rearrange("p (t s) -> p t s", t=PACK)
+        z2_room = pair_room[:, LAST * S :]
 
         def pair_product(t):
             nc.vector.tensor_tensor(pair[:, t, :], y_win[t][:].indirect(n1_sb[:]), y_plain[:, t, :], ALU.mult)
 
-        for t in range(PACK - 1):
+        for t in range(LAST):
             pair_product(t)
-        y_gm = planes("y_gm")
+        y_gm = keep.tile([P, PACK, S], F32, name="y_gm")
         for t in range(PACK):
             nc.vector.tensor_scalar(y_gm[:, t, :], y_plain[:, t, :], gm_sb[:, t : t + 1], None, ALU.mult)
-        w3_dealt = deal_weight("w3", w3_raw, [nc.scalar.copy], "st_win2")
-        z2_q = quantize("z2", [weave(nc.vector, pair_room[:, (PACK - 1) * S :], h, gate, y_gm) for h in range(2)])
-        w3_q = quantize("w3", w3_dealt)
-        pair_product(PACK - 1)
+        w3_dealt = deal_weight("w3", w3_raw, [nc.scalar.copy], f"st_win{LAST - 1}")
+        z2_q = quantize("z2", [weave(nc.vector, z2_room, half, gate, y_gm) for half in HALVES])
+        w3_q = quantize("w3", [w3_dealt])
+        pair_product(LAST)
 
         b_win = windows("b_win")
         for t in range(PACK):
-            acc = product(PACK + t, t, w3_q, z2_q)
-            nc.scalar.copy(b_win[t][:, 0:S], acc[:])
+            acc = product(PACK + t, t, w3_q, z2_q, ALL)
+            nc.scalar.copy(b_win[t][:, ALL], acc[:])
 
         gn_twice = keep.tile([P, PACK], F32, name="gn_twice")
         nc.gpsimd.tensor_scalar(gn_twice[:], gn_sb[:], 2.0, 0.0, ALU.mult, ALU.add)
@@ -170,45 +180,71 @@ def tile_picked_forkclampbcubehopd_none_p_kernel(tc, x_words, x_scales, w1, gn, 
             keep.tile([P, PACK, S // 2], F32, name="sig1", tag="z2_codes", align_bytes=64),
         ]
         tanh_gn = keep.tile([P, PACK, S], F32, name="tanh_gn", tag="y_plain")
-        low_room = keep.tile([P, PACK * S], F32, name="low_room", align_bytes=64)
-        low = [low_room[:, t * S : (t + 1) * S] for t in range(PACK)]
-        for h, half in enumerate(halves):
-            for t in range(PACK):
-                entries = n2_sb[:, half.start // 16 : half.stop // 16]
-                nc.scalar.activation(sig[h][:, t, :], y_win[t][:].indirect(entries), ACT.Sigmoid, scale=2.0)
-                nc.gpsimd.tensor_scalar(
-                    tanh_gn[:, t, half], sig[h][:, t, :], gn_twice[:, t : t + 1], gn_minus[:, t : t + 1], ALU.mult, ALU.add
-                )
-            weave(nc.gpsimd, low_room[:, 2 * S :], h, pair, tanh_gn)
-        w2_dealt = deal_weight("w2", w2_raw, [nc.scalar.copy], "y_win2")
-        cap = planes("cap")
         for t in range(PACK):
-            nc.vector.tensor_copy(cap[:, t, :], b_win[t][:].indirect(n6_sb[:]))
-        w2_q = quantize("w2", w2_dealt)
-        z_q = quantize("z", [low_room[:, 2 * S :].bitcast(BF16)])
+            nc.scalar.activation(
+                sig[0][:, t, :], y_win[t][:].indirect(entries_for(n2_sb, HALVES[0])), ACT.Sigmoid, scale=2.0
+            )
+            nc.gpsimd.tensor_scalar(
+                tanh_gn[:, t, HALVES[0]],
+                sig[0][:, t, :],
+                gn_twice[:, t : t + 1],
+                gn_minus[:, t : t + 1],
+                ALU.mult,
+                ALU.add,
+            )
         for t in range(PACK):
-            nc.vector.tensor_copy(low[t], b_win[t][:].indirect(n7_sb[:]))
+            nc.scalar.activation(
+                sig[1][:, t, :], y_win[t][:].indirect(entries_for(n2_sb, HALVES[1])), ACT.Sigmoid, scale=2.0
+            )
+            nc.scalar.activation(
+                tanh_gn[:, t, HALVES[1]],
+                sig[1][:, t, :],
+                ACT.Identity,
+                scale=gn_twice[:, t : t + 1],
+                bias=gn_minus[:, t : t + 1],
+            )
+        z_room = keep.tile([P, 2 * S], F32, name="z_room", align_bytes=64)
+        weave(nc.gpsimd, z_room[:], HALVES[0], pair, tanh_gn)
+        weave(nc.gpsimd, z_room[:], THIRD_QUARTER, pair, tanh_gn)
+        w2_dealt = deal_weight("w2", w2_raw, [nc.scalar.copy], "z2_codes")
+
+        b_n6 = keep.tile([P, PACK, S], F32, name="b_n6")
+        for t in range(PACK):
+            nc.vector.tensor_copy(b_n6[:, t, :], b_win[t][:].indirect(n6_sb[:]))
+        b_n7_early = keep.tile([P, 2 * S], F32, name="b_n7_early")
+        b_n7 = [b_n7_early[:, 0:S], b_n7_early[:, S:]]
+        for t in range(PACK // 2):
+            nc.vector.tensor_copy(b_n7[t], b_win[t][:].indirect(n7_sb[:]))
+        weave(nc.vector, z_room[:], LAST_QUARTER, pair, tanh_gn)
+        w2_q = quantize("w2", [w2_dealt])
+        z_q = quantize("z", [z_room[:].bitcast(BF16)])
+        b_n7_late = keep.tile([P, 2 * S], F32, name="b_n7_late", tag="z2_codes", align_bytes=64)
+        b_n7.extend([b_n7_late[:, 0:S], b_n7_late[:, S:]])
+        for t in range(PACK // 2, PACK):
+            nc.vector.tensor_copy(b_n7[t], b_win[t][:].indirect(n7_sb[:]))
 
         a_win = windows("a_win")
-        a_plain = planes("a_plain")
-        out_rows = out.rearrange("(p t) s -> p t s", t=PACK)
+        a_plain = keep.tile([P, PACK, S], F32, name="a_plain")
         for t in range(PACK):
-            acc = product(t, t, w2_q, z_q)
-            nc.scalar.activation(a_win[t][:, 0:S], acc[:], ACT.Copy, scale=-0.5)
+            acc = product(t, t, w2_q, z_q, ALL)
+            nc.scalar.activation(a_win[t][:, ALL], acc[:], ACT.Copy, scale=-0.5)
             nc.scalar.copy(a_plain[:, t, :], acc[:])
-        diff = keep.tile([P, PACK, S], F32, name="diff", tag="z_codes", align_bytes=64)
+        result = keep.tile([P, PACK, S], F32, name="result", tag="z_codes", align_bytes=64)
+        out_rows = out.rearrange("(p t) s -> p t s", t=PACK)
 
-        def hop(t):
-            nc.vector.tensor_tensor(diff[:, t, :], a_win[t][:].indirect(n5_sb[:]), a_plain[:, t, :], ALU.add)
+        def less_half(t):
+            nc.vector.tensor_tensor(result[:, t, :], a_win[t][:].indirect(n5_sb[:]), a_plain[:, t, :], ALU.add)
 
         def smaller(t):
-            nc.vector.tensor_tensor(diff[:, t, :], diff[:, t, :], cap[:, t, :], ALU.min)
+            nc.vector.tensor_tensor(result[:, t, :], result[:, t, :], b_n6[:, t, :], ALU.min)
 
         def larger(t):
-            nc.vector.tensor_tensor(diff[:, t, :], diff[:, t, :], low[t], ALU.max)
-            nc.sync.dma_start(out_rows[:, t, :], diff[:, t, :])
+            for places, queue in zip(HALVES, (nc.sync, nc.scalar)) if t == LAST else [(ALL, nc.sync)]:
+                nc.vector.tensor_tensor(result[:, t, places], result[:, t, places], b_n7[t][:, places], ALU.max)
+                queue.dma_start(out_rows[:, t, places], result[:, t, places])
 
-        for step in range(PACK + 2):
-            for stage, lag in ((hop, 0), (smaller, 1), (larger, 2)):
+        stages = (less_half, smaller, larger)
+        for step in range(PACK + len(stages) - 1):
+            for lag, stage in enumerate(stages):
                 if 0 <= step - lag < PACK:
                     stage(step - lag)

@@ -25,8 +25,6 @@ WINDOW = 2 * S
 RUN = 4
 ALL = slice(0, S)
 HALVES = (slice(0, S // 2), slice(S // 2, S))
-THIRD_QUARTER = slice(S // 2, 3 * S // 4)
-LAST_QUARTER = slice(3 * S // 4, S)
 
 
 def tile_picked_forkclampbcubehopd_none_p_kernel(
@@ -105,8 +103,11 @@ def tile_picked_forkclampbcubehopd_none_p_kernel(
             )
             return woven
 
+        warm = keep.tile([P, 2], F32, name="warm")
+        nc.gpsimd.memset(warm[:, 0:1], 0.0)
         x_scale_table = keep.tile([P, T], U8, name="x_scale_table", align_bytes=64)
         nc.gpsimd.memset(x_scale_table[:].bitcast(I32), 0)
+        nc.scalar.activation(warm[:, 1:2], warm[:, 0:1], ACT.Sigmoid)
         offs_sb = load_list("offs_sb", offs)
         for q in range(P // QUADRANT):
             nc.sync.dma_start(
@@ -180,46 +181,37 @@ def tile_picked_forkclampbcubehopd_none_p_kernel(
             keep.tile([P, PACK, S // 2], F32, name="sig1", tag="z2_codes", align_bytes=64),
         ]
         tanh_gn = keep.tile([P, PACK, S], F32, name="tanh_gn", tag="y_plain")
-        for t in range(PACK):
-            nc.scalar.activation(
-                sig[0][:, t, :], y_win[t][:].indirect(entries_for(n2_sb, HALVES[0])), ACT.Sigmoid, scale=2.0
-            )
-            nc.gpsimd.tensor_scalar(
-                tanh_gn[:, t, HALVES[0]],
-                sig[0][:, t, :],
-                gn_twice[:, t : t + 1],
-                gn_minus[:, t : t + 1],
-                ALU.mult,
-                ALU.add,
-            )
-        for t in range(PACK):
-            nc.scalar.activation(
-                sig[1][:, t, :], y_win[t][:].indirect(entries_for(n2_sb, HALVES[1])), ACT.Sigmoid, scale=2.0
-            )
-            nc.scalar.activation(
-                tanh_gn[:, t, HALVES[1]],
-                sig[1][:, t, :],
-                ACT.Identity,
-                scale=gn_twice[:, t : t + 1],
-                bias=gn_minus[:, t : t + 1],
-            )
+
+        def tanh_factors(h):
+            for t in range(PACK):
+                nc.scalar.activation(
+                    sig[h][:, t, :], y_win[t][:].indirect(entries_for(n2_sb, HALVES[h])), ACT.Sigmoid, scale=2.0
+                )
+                nc.gpsimd.tensor_scalar(
+                    tanh_gn[:, t, HALVES[h]],
+                    sig[h][:, t, :],
+                    gn_twice[:, t : t + 1],
+                    gn_minus[:, t : t + 1],
+                    ALU.mult,
+                    ALU.add,
+                )
+
         z_room = keep.tile([P, 2 * S], F32, name="z_room", align_bytes=64)
+        tanh_factors(0)
         weave(nc.gpsimd, z_room[:], HALVES[0], pair, tanh_gn)
-        weave(nc.gpsimd, z_room[:], THIRD_QUARTER, pair, tanh_gn)
-        w2_dealt = deal_weight("w2", w2_raw, [nc.scalar.copy], "z2_codes")
+        tanh_factors(1)
+        w2_dealt = deal_weight("w2", w2_raw, [nc.scalar.copy], f"y_win{LAST - 1}")
 
         b_n6 = keep.tile([P, PACK, S], F32, name="b_n6")
         for t in range(PACK):
             nc.vector.tensor_copy(b_n6[:, t, :], b_win[t][:].indirect(n6_sb[:]))
         b_n7_early = keep.tile([P, 2 * S], F32, name="b_n7_early")
-        b_n7 = [b_n7_early[:, 0:S], b_n7_early[:, S:]]
+        b_n7 = [b_n7_early[:, 0:S], b_n7_early[:, S:], z_room[:, 0:S], z_room[:, S:]]
         for t in range(PACK // 2):
             nc.vector.tensor_copy(b_n7[t], b_win[t][:].indirect(n7_sb[:]))
-        weave(nc.vector, z_room[:], LAST_QUARTER, pair, tanh_gn)
+        weave(nc.vector, z_room[:], HALVES[1], pair, tanh_gn)
         w2_q = quantize("w2", [w2_dealt])
         z_q = quantize("z", [z_room[:].bitcast(BF16)])
-        b_n7_late = keep.tile([P, 2 * S], F32, name="b_n7_late", tag="z2_codes", align_bytes=64)
-        b_n7.extend([b_n7_late[:, 0:S], b_n7_late[:, S:]])
         for t in range(PACK // 2, PACK):
             nc.vector.tensor_copy(b_n7[t], b_win[t][:].indirect(n7_sb[:]))
 

from contextlib import ExitStack

import concourse.mybir as mybir

K, T, S, N, H = 512, 2048, 512, 512, 512
FLOPS = 2 * S * (K * H + 2 * H * N)

F32 = mybir.dt.float32
BF16 = mybir.dt.bfloat16
I32 = mybir.dt.int32
U32 = mybir.dt.uint32
U16 = mybir.dt.uint16
U8 = mybir.dt.uint8
FP8X4 = mybir.dt.float8_e4m3fn_x4
ALU = mybir.AluOpType
ACT = mybir.ActivationFunctionType

P = 128
PACK = 4
LAST = PACK - 1
WIDTH = 512
GROUP = 16
QUADRANT = 32
WINDOW = 2 * S
RUN = 4
ALL = slice(0, S)
HALVES = (slice(0, S // 2), slice(S // 2, S))


def tile_picked_forkclampbcubehopd_none_p_kernel(
    tc, x_words, x_scales, w1, gn, w2, gm, w3, offs, n1, n2, n3, n4, n5, n6, n7, out
):
    nc = tc.nc
    with ExitStack() as ctx:
        keep = ctx.enter_context(tc.tile_pool(name="keep", bufs=1))
        psum = ctx.enter_context(tc.psum_pool(name="psum", bufs=1))

        def load_list(name, src):
            entries = keep.tile([P, S // GROUP], U16, name=name)
            nc.sync.dma_start(entries[:], src)
            return entries

        def entries_for(entries, places):
            return entries[:, places.start // GROUP : places.stop // GROUP]

        def load_gain(name, gain):
            per_plane = keep.tile([P, PACK], F32, name=name)
            nc.sync.dma_start(per_plane[:], gain.rearrange("(p t) o -> p (t o)", t=PACK))
            return per_plane

        def load_weight(name, w, pieces):
            width = WIDTH // pieces
            raws = []
            for h in range(pieces):
                raw = keep.tile([P, PACK, width], F32, name=f"{name}_raw{h}")
                nc.sync.dma_start(raw[:], w.rearrange("(p j) c -> p j c", j=PACK)[:, :, h * width : (h + 1) * width])
                raws.append(raw)
            return raws

        def deal_weight(name, raws, copies, tag):
            dealt = keep.tile([P, PACK, P, PACK], BF16, name=f"{name}_dealt", tag=tag, align_bytes=64)
            span = P // len(raws)
            for h, raw in enumerate(raws):
                copies[h](
                    dealt[:, :, h * span : (h + 1) * span, :].rearrange("p t m j -> p m j t"),
                    raw[:].rearrange("p j (m t) -> p m j t", t=PACK),
                )
            return dealt[:].rearrange("p t m j -> p (t m j)")

        def quantize(name, pieces):
            codes = keep.tile([P, WIDTH], U32, name=f"{name}_codes", tag=f"{name}_codes", align_bytes=64)
            scales = keep.tile([P, WIDTH], U8, name=f"{name}_scales", align_bytes=64)
            width = WIDTH // len(pieces)
            for h, piece in enumerate(pieces):
                cols = slice(h * width, (h + 1) * width)
                nc.vector.quantize_mx(out=codes[:, cols].bitcast(FP8X4), scales=scales[:, cols], in_=piece)
            return codes, scales

        def product(bank, t, weight, moving, places):
            acc = psum.tile([P, places.stop - places.start], F32, name=f"bank{bank}", tag=f"bank{bank}")
            cols = slice(t * P, (t + 1) * P)
            nc.tensor.matmul_mx(
                out=acc[:],
                lhsT=weight[0][:, cols].bitcast(FP8X4),
                lhsT_scale=weight[1][:, cols],
                rhs=moving[0][:, places].bitcast(FP8X4),
                rhs_scale=moving[1][:, places],
                start=True,
                stop=True,
            )
            return acc

        def windows(name):
            return [keep.tile([P, WINDOW], F32, name=f"{name}{t}", tag=f"{name}{t}", align_bytes=64) for t in range(PACK)]

        def weave(engine, room, places, left, right):
            woven = room.bitcast(BF16)[:, PACK * places.start : PACK * places.stop]
            engine.tensor_tensor(
                woven.rearrange("p (c i t) -> p c t i", i=RUN, t=PACK),
                left[:, :, places].rearrange("p t (c i) -> p c t i", i=RUN),
                right[:, :, places].rearrange("p t (c i) -> p c t i", i=RUN),
                ALU.mult,
            )
            return woven

        warm = keep.tile([P, 2], F32, name="warm")
        nc.gpsimd.memset(warm[:, 0:1], 0.0)
        x_scale_table = keep.tile([P, T], U8, name="x_scale_table", align_bytes=64)
        nc.gpsimd.memset(x_scale_table[:].bitcast(I32), 0)
        nc.scalar.activation(warm[:, 1:2], warm[:, 0:1], ACT.Sigmoid)
        offs_sb = load_list("offs_sb", offs)
        for q in range(P // QUADRANT):
            nc.sync.dma_start(
                x_scale_table[QUADRANT * q : QUADRANT * q + PACK, :].bitcast(I32),
                x_scales[0, PACK * q : PACK * (q + 1), :].bitcast(I32),
            )
        w1_raw = load_weight("w1", w1, 2)
        x_word_table = keep.tile([P, T], U32, name="x_word_table", align_bytes=64)
        nc.sync.dma_start(x_word_table[:].bitcast(I32), x_words[0].rearrange("p n t -> p (n t)").bitcast(I32))
        n3_sb = load_list("n3_sb", n3)
        n1_sb = load_list("n1_sb", n1)
        n4_sb = load_list("n4_sb", n4)
        gm_sb = load_gain("gm_sb", gm)
        w3_raw = load_weight("w3", w3, 1)
        gn_sb = load_gain("gn_sb", gn)
        n2_sb = load_list("n2_sb", n2)
        w2_raw = load_weight("w2", w2, 1)
        n6_sb = load_list("n6_sb", n6)
        n7_sb = load_list("n7_sb", n7)
        n5_sb = load_list("n5_sb", n5)

        x_scale = keep.tile([P, S], U8, name="x_scale", align_bytes=64)
        nc.vector.tensor_copy(x_scale[:], x_scale_table[:].indirect(offs_sb[:]))
        w1_q = quantize("w1", [deal_weight("w1", w1_raw, [nc.scalar.copy, nc.vector.tensor_copy], "w1_dealt")])
        x_word = keep.tile([P, S], U32, name="x_word", align_bytes=64)
        for half in HALVES:
            nc.vector.tensor_copy(x_word[:, half], x_word_table[:].indirect(entries_for(offs_sb, half)))

        y_win = windows("y_win")
        st_win = windows("st_win")
        y_plain = keep.tile([P, PACK, S], F32, name="y_plain", tag="y_plain")
        for t in range(PACK):
            for part, places in enumerate(HALVES if t == 0 else [ALL]):
                acc = product(part * PACK + t, t, w1_q, (x_word, x_scale), places)
                nc.scalar.copy(y_win[t][:, places], acc[:])
                nc.scalar.copy(y_plain[:, t, places], acc[:])
            nc.vector.tensor_tensor(st_win[t][:, ALL], y_win[t][:].indirect(n3_sb[:]), y_plain[:, t, :], ALU.subtract)

        gate = keep.tile([P, PACK, S], F32, name="gate")
        for t in range(PACK):
            nc.scalar.activation(gate[:, t, :], st_win[t][:].indirect(n4_sb[:]), ACT.Sigmoid)

        pair_room = keep.tile([P, (PACK + 1) * S], F32, name="pair_room", align_bytes=64)
        pair = pair_room[:, 0 : PACK * S].rearrange("p (t s) -> p t s", t=PACK)
        z2_room = pair_room[:, LAST * S :]

        def pair_product(t):
            nc.vector.tensor_tensor(pair[:, t, :], y_win[t][:].indirect(n1_sb[:]), y_plain[:, t, :], ALU.mult)

        for t in range(LAST):
            pair_product(t)
        y_gm = keep.tile([P, PACK, S], F32, name="y_gm")
        for t in range(PACK):
            nc.vector.tensor_scalar(y_gm[:, t, :], y_plain[:, t, :], gm_sb[:, t : t + 1], None, ALU.mult)
        w3_dealt = deal_weight("w3", w3_raw, [nc.scalar.copy], f"st_win{LAST - 1}")
        z2_q = quantize("z2", [weave(nc.vector, z2_room, half, gate, y_gm) for half in HALVES])
        w3_q = quantize("w3", [w3_dealt])
        pair_product(LAST)

        b_win = windows("b_win")
        for t in range(PACK):
            acc = product(PACK + t, t, w3_q, z2_q, ALL)
            nc.scalar.copy(b_win[t][:, ALL], acc[:])

        gn_twice = keep.tile([P, PACK], F32, name="gn_twice")
        nc.gpsimd.tensor_scalar(gn_twice[:], gn_sb[:], 2.0, 0.0, ALU.mult, ALU.add)
        gn_minus = keep.tile([P, PACK], F32, name="gn_minus")
        nc.gpsimd.tensor_scalar(gn_minus[:], gn_sb[:], -1.0, 0.0, ALU.mult, ALU.add)
        sig = [
            keep.tile([P, PACK, S // 2], F32, name="sig0"),
            keep.tile([P, PACK, S // 2], F32, name="sig1", tag="z2_codes", align_bytes=64),
        ]
        tanh_gn = keep.tile([P, PACK, S], F32, name="tanh_gn", tag="y_plain")

        def tanh_factors(h):
            for t in range(PACK):
                nc.scalar.activation(
                    sig[h][:, t, :], y_win[t][:].indirect(entries_for(n2_sb, HALVES[h])), ACT.Sigmoid, scale=2.0
                )
                nc.gpsimd.tensor_scalar(
                    tanh_gn[:, t, HALVES[h]],
                    sig[h][:, t, :],
                    gn_twice[:, t : t + 1],
                    gn_minus[:, t : t + 1],
                    ALU.mult,
                    ALU.add,
                )

        z_room = keep.tile([P, 2 * S], F32, name="z_room", align_bytes=64)
        tanh_factors(0)
        weave(nc.gpsimd, z_room[:], HALVES[0], pair, tanh_gn)
        tanh_factors(1)
        w2_dealt = deal_weight("w2", w2_raw, [nc.scalar.copy], f"y_win{LAST - 1}")

        b_n6 = keep.tile([P, PACK, S], F32, name="b_n6")
        for t in range(PACK):
            nc.vector.tensor_copy(b_n6[:, t, :], b_win[t][:].indirect(n6_sb[:]))
        b_n7_early = keep.tile([P, 2 * S], F32, name="b_n7_early")
        b_n7 = [b_n7_early[:, 0:S], b_n7_early[:, S:], z_room[:, 0:S], z_room[:, S:]]
        for t in range(PACK // 2):
            nc.vector.tensor_copy(b_n7[t], b_win[t][:].indirect(n7_sb[:]))
        weave(nc.vector, z_room[:], HALVES[1], pair, tanh_gn)
        w2_q = quantize("w2", [w2_dealt])
        z_q = quantize("z", [z_room[:].bitcast(BF16)])
        for t in range(PACK // 2, PACK):
            nc.vector.tensor_copy(b_n7[t], b_win[t][:].indirect(n7_sb[:]))

        a_win = windows("a_win")
        a_plain = keep.tile([P, PACK, S], F32, name="a_plain")
        for t in range(PACK):
            acc = product(t, t, w2_q, z_q, ALL)
            nc.scalar.activation(a_win[t][:, ALL], acc[:], ACT.Copy, scale=-0.5)
            nc.scalar.copy(a_plain[:, t, :], acc[:])
        result = keep.tile([P, PACK, S], F32, name="result", tag="z_codes", align_bytes=64)
        out_rows = out.rearrange("(p t) s -> p t s", t=PACK)

        def less_half(t):
            nc.vector.tensor_tensor(result[:, t, :], a_win[t][:].indirect(n5_sb[:]), a_plain[:, t, :], ALU.add)

        def smaller(t):
            nc.vector.tensor_tensor(result[:, t, :], result[:, t, :], b_n6[:, t, :], ALU.min)

        def larger(t):
            for places, queue in zip(HALVES, (nc.sync, nc.scalar)) if t == LAST else [(ALL, nc.sync)]:
                nc.vector.tensor_tensor(result[:, t, places], result[:, t, places], b_n7[t][:, places], ALU.max)
                queue.dma_start(out_rows[:, t, places], result[:, t, places])

        stages = (less_half, smaller, larger)
        for step in range(PACK + len(stages) - 1):
            for lag, stage in enumerate(stages):
                if 0 <= step - lag < PACK:
                    stage(step - lag)
